import numpy as np, ml_dtypes
CORES = [33,38,57,62,81,86,161,166,185,190,209,214]
N = 12
import mx_ref
NC, G = 128, 4
C = np.float32(0.037)
BF = ml_dtypes.bfloat16
def cut(t, i, w=512):
    return t[:, w * i:w * i + w]
def tile(rs):
    return np.stack(rs, axis=2).reshape(128, -1).astype(BF)
def layer(w, X):
    out = []
    for i in range(G):
        for t in range(len(X)):
            p = mx_ref.matmul(mx_ref.quantize(cut(w, len(X) * i + t)), X[t])
            z = p if t == 0 else z + p
        out.append(z)
    return out
def rot(Z, c, s):
    return [(Z[0] * c - Z[1] * s) * C, (Z[0] * s + Z[1] * c) * C, (Z[2] * c - Z[3] * s) * C, (Z[2] * s + Z[3] * c) * C]
def setup_inputs(rng):
    def f(*shape):
        return mx_ref.flush((rng.standard_normal(shape, dtype=np.float32) * np.exp2(rng.integers(-2, 3, shape[:-1] + (1,)))).astype(BF))
    ang = rng.random((N, 128, 128)) * (2 * np.pi)
    return {"cs": np.cos(ang).astype(BF), "sn": np.sin(ang).astype(BF), "xk": f(N, 128, 512), "wk": f(N, 128, G * 512), "xq": f(N, 128, 4 * NC)}
def setup_inputs_blocks(rng):
    d = setup_inputs(rng)
    for k in ("xk", "wk", "xq"): d[k] = mx_ref.spread(d[k], rng, 4)
    return d
def setup_inputs_wide(rng):
    d = setup_inputs(rng)
    for k in ("xk", "wk", "xq"): d[k] = mx_ref.flush((d[k].astype(np.float32) * np.exp2(rng.integers(-5, 6, (N, 1, 1))).astype(np.float32)).astype(BF))
    return d
def setup_inputs_zeros(rng):
    d = setup_inputs(rng); v = d["xk"].reshape(N, 128, -1, 4).copy()
    v[np.broadcast_to((rng.random((N, 1, v.shape[2], 1)) < 0.33), v.shape)] = 0
    d["xk"] = v.reshape(d["xk"].shape)
    return d
def reference(cs, sn, xk, wk, xq):
    K = [mx_ref.quantize(tile(rot(layer(wk[j], [mx_ref.quantize(xk[j])]), cs[j].astype(np.float32), sn[j].astype(np.float32)))) for j in range(N)]
    y = np.zeros((N, 128, N * NC), np.float32)
    for r in range(N):
        q = mx_ref.quantize(xq[r])
        for j in range(N):
            y[r][:, NC * j:NC * j + NC] = mx_ref.matmul(K[j], q)
    return {"y": y}

from concourse.bass import DstId, RemoteDMATransfer
from concourse.mybir import dt, AluOpType, ActivationFunctionType

N, W, WORLD = 12, 128, 256
SCALE = 0.037

SCRATCH = {
    "xks": ("sbuf", [128, 512], "bfloat16"),
    "wks": ("sbuf", [128, 2048], "bfloat16"),
    "xqs": ("sbuf", [128, 512], "bfloat16"),
    "css": ("sbuf", [128, 128], "bfloat16"),
    "sns": ("sbuf", [128, 128], "bfloat16"),
    "xkc": ("sbuf", [128, 128], "float8_e4m3fn_x4"),
    "xkp": ("sbuf", [128, 128], "uint8"),
    "wkc": ("sbuf", [128, 512], "float8_e4m3fn_x4"),
    "wkp": ("sbuf", [128, 512], "uint8"),
    "xqc": ("sbuf", [128, 128], "float8_e4m3fn_x4"),
    "xqp": ("sbuf", [128, 128], "uint8"),
    "prod": ("sbuf", [128, 1024], "float32"),
    "rsum": ("sbuf", [128, 512], "float32"),
    "kt": ("sbuf", [128, 512], "bfloat16"),
    "kc": ("sbuf", [128, N * W], "float8_e4m3fn_x4"),
    "kp": ("sbuf", [128, N * W], "uint8"),
    "yb": ("sbuf", [128, N * W], "float32"),
    "ps": ("psum", [128, 4096], "float32"),
}
SEMAPHORES = (["lxk", "lcs", "lxq", "qxk", "qxq", "qk", "kts", "snd", "st"]
              + [n + "%d" % i for n in ("lw", "qw", "z", "pr", "s") for i in range(4)]
              + [n + "%d" % i for n in ("c", "p", "m", "y") for i in range(N)])


def make_plan(cores, topo):
    def same_chip(a, b):
        return topo.host(a) == topo.host(b) and topo.chip(a) == topo.chip(b)

    ranks = range(len(cores))
    chips = []
    for r in ranks:
        for ch in chips:
            if same_chip(cores[ch[0]], cores[r]):
                ch.append(r)
                break
        else:
            chips.append([r])
    n = len(chips)
    chip_of = {r: i for i, ch in enumerate(chips) for r in ch}
    peer = {r: [q for q in chips[chip_of[r]] if q != r][0] for r in ranks}

    ALL = topo.mask(cores[0], cores[peer[0]])
    OUT = [topo.mask(cores[0], c) for c in cores if topo.same_plane(cores[0], c)][0]
    INN = ALL & ~OUT

    def twin(s, j):
        return [r for r in chips[j] if topo.die(cores[r]) == topo.die(cores[s])][0]

    near, late, lent, helpers = {}, {}, {}, {}
    for s in ranks:
        to = [twin(s, (chip_of[s] + k) % n) for k in range(1, n)]
        near[s] = [d for d in to if topo.may_write(cores[s], cores[d])]
        late[s] = [d for d in to if d not in near[s]]
        lent[s], helpers[s] = [], []
        if late[s]:
            helpers[s] = [h for h in range(WORLD) if h not in cores and same_chip(h, cores[s])
                          and topo.die(h) == topo.die(cores[s])
                          and all(topo.may_write(h, cores[d]) for d in late[s])][:(len(late[s]) + 1) // 2]
        else:
            d = to[n // 2 - 1]
            near[s].remove(d)
            lent[s] = [twin(peer[s], chip_of[d])]

    calls = {c: [] for c in range(WORLD)}
    for s in ranks:
        me = cores[s]
        inn = (INN, [s], helpers[s] + [cores[peer[s]]])
        out = (OUT, [s], [cores[d] for d in near[s]])
        if helpers[s]:
            calls[me] += [("p", [s], [inn]), ("c", [s], [inn]), ("p", [s], [out]), ("c", [s], [out])]
        else:
            calls[me] += [("p", [s], [inn, out]), ("c", [s], [inn, out])]
        for i, h in enumerate(helpers[s]):
            to = [cores[d] for d in late[s][i::len(helpers[s])]]
            calls[h] += [(x, [s], [(OUT, [s], to)]) for x in "pc"]
    for r in ranks:
        p = peer[r]
        if lent[p]:
            calls[cores[r]] += [(x, [p], [(OUT, [p], [cores[d] for d in lent[p]])]) for x in "cp"]

    land = {}
    for r in ranks:
        src = [twin(r, (chip_of[r] - k) % n) for k in range(1, n)]
        land[r] = ([s for s in src if r in near[s]], [s for s in ranks if r in lent[s]], [s for s in src if r in late[s]])
    slots, seqs = {}, {}
    for r in ranks:
        a, lo, la = land[r]
        groups = [a, lo, la[:2], la[2:]] if lo else [a[:2], a[2:], la]
        for i, gr in enumerate(gr for gr in groups if gr):
            calls[cores[r]] += [(x, gr, [(ALL if i else INN, gr, [cores[peer[r]]])]) for x in "cp"]
        slots[cores[r]] = {}
        for q in chips[chip_of[r]]:
            for s in land[q][0] + land[q][1] + land[q][2] + [q]:
                slots[cores[r]][s] = len(slots[cores[r]])
        b = land[peer[r]]
        seqs[r] = [r, peer[r]] + a + b[0] + lo + b[1] + la + b[2]

    arrive = {}
    for c in calls:
        for kind, _, parts in calls[c]:
            for m, tiles, ds in parts:
                for d in ds:
                    for t in tiles:
                        arrive[d, kind, t] = (kind + "%d" % tiles[0], bin(m).count("1"))
    return {"calls": calls, "slots": slots, "arrive": arrive, "seqs": seqs}


def rank_program(g, core, T, topo):
    cores = list(T.cores)
    plan = make_plan(cores, topo)
    rank = T.rank_of(core)
    sem = T.sem
    arrive = plan["arrive"]

    def col(c, t):
        return W * plan["slots"][c][t] if c in plan["slots"] else 0

    def view(kind, a, n):
        return T.kc[:, a:a + n].bitcast(dt.uint8) if kind == "c" else T.kp[:, a:a + n]

    def dst_id(d):
        rid, pid = topo.addr(d, core)
        return DstId(rid=rid, pnc=pid)

    def talk():
        sent = 0
        for kind, waits, parts in plan["calls"][core]:
            for t in waits:
                if t == rank:
                    g.wait_ge(sem["qk"], 1)
                else:
                    name, n = arrive[core, kind, t]
                    g.wait_ge(sem[name], n)
            trs = []
            for m, tiles, ds in parts:
                n = W * len(tiles)
                trs.append(RemoteDMATransfer(dst_ids=[dst_id(d) for d in ds], dma_engine_mask=m,
                                             remote_sem=sem[kind + "%d" % tiles[0]],
                                             srcs=[view(kind, col(core, tiles[0]), n)],
                                             dsts=[view(kind, col(d, tiles[0]), n) for d in ds]))
                sent += bin(m).count("1")
            g.remote_dma_fused(trs, local_sem=sem["snd"])
        g.wait_ge(sem["snd"], sent)

    if rank is None:
        if plan["calls"][core]:
            talk()
        return

    own = col(core, rank)
    g.sync.dma_start(T.xks[:], T.xk[:]).then_inc(sem["lxk"], 16)
    g.scalar.dma_start(T.wks[:, 0:512], T.wk[:, 0:512]).then_inc(sem["lw0"], 16)
    g.sync.dma_start(T.wks[:, 512:1024], T.wk[:, 512:1024]).then_inc(sem["lw1"], 16)
    g.scalar.dma_start(T.css[:], T.cs[:]).then_inc(sem["lcs"], 16)
    g.scalar.dma_start(T.sns[:], T.sn[:]).then_inc(sem["lcs"], 16)
    g.sync.dma_start(T.wks[:, 1024:1536], T.wk[:, 1024:1536]).then_inc(sem["lw2"], 16)
    g.scalar.dma_start(T.wks[:, 1536:2048], T.wk[:, 1536:2048]).then_inc(sem["lw3"], 16)
    g.sync.wait_ge(sem["lw3"], 16)
    g.sync.dma_start(T.xqs[:], T.xq[:]).then_inc(sem["lxq"], 16)

    v, te, sc = g.vector, g.tensor, g.scalar
    v.wait_ge(sem["lxk"], 16)
    v.quantize_mx(T.xkc[:], T.xkp[:], T.xks[:]).then_inc(sem["qxk"], 1)
    te.wait_ge(sem["qxk"], 1)
    for i in range(4):
        te.wait_ge(sem["qw%d" % i], 1)
        te.matmul_mx(T.ps[:, 512 * i:512 * i + W], T.wkc[:, W * i:W * i + W], T.wkp[:, W * i:W * i + W],
                     T.xkc[:], T.xkp[:], True, True).then_inc(sem["z%d" % i], 1)

    def qw(i):
        v.wait_ge(sem["lw%d" % i], 16)
        v.quantize_mx(T.wkc[:, W * i:W * i + W], T.wkp[:, W * i:W * i + W],
                      T.wks[:, 512 * i:512 * i + 512]).then_inc(sem["qw%d" % i], 1)

    def prod(k):
        return T.prod[:, W * k:W * k + W]

    def mul(i, k, t):
        v.tensor_tensor(prod(k), T.ps[:, 512 * i:512 * i + W], t[:], AluOpType.mult).then_inc(sem["pr%d" % (k // 2)], 1)

    def muls(h):
        v.wait_ge(sem["z%d" % (2 * h)], 1)
        mul(2 * h, 4 * h, T.css)
        mul(2 * h, 4 * h + 2, T.sns)
        v.wait_ge(sem["z%d" % (2 * h + 1)], 1)
        mul(2 * h + 1, 4 * h + 1, T.sns)
        mul(2 * h + 1, 4 * h + 3, T.css)

    def addsub(i):
        v.wait_ge(sem["pr%d" % i], 2)
        v.tensor_tensor(T.rsum[:, W * i:W * i + W], prod(2 * i), prod(2 * i + 1),
                        AluOpType.add if i % 2 else AluOpType.subtract).then_inc(sem["s%d" % i], 1)

    qw(0)
    qw(1)
    v.wait_ge(sem["lcs"], 32)
    muls(0)
    qw(2)
    addsub(0)
    qw(3)
    addsub(1)
    muls(1)
    addsub(2)
    addsub(3)
    for i in range(4):
        sc.wait_ge(sem["s%d" % i], 1)
        sc.activation(T.kt[:, i:512:4], T.rsum[:, W * i:W * i + W], ActivationFunctionType.Identity,
                      scale=SCALE).then_inc(sem["kts"], 1)
    v.wait_ge(sem["kts"], 4)
    v.quantize_mx(T.kc[:, own:own + W], T.kp[:, own:own + W], T.kt[:]).then_inc(sem["qk"], 1)
    v.wait_ge(sem["lxq"], 16)
    v.quantize_mx(T.xqc[:], T.xqp[:], T.xqs[:]).then_inc(sem["qxq"], 1)

    talk()

    te.wait_ge(sem["qk"], 1)
    te.wait_ge(sem["qxq"], 1)
    for i, s in enumerate(plan["seqs"][rank]):
        a, bank = col(core, s), 512 * ((4 + i) % 8)
        if s != rank:
            for kind in "pc":
                name, n = arrive[core, kind, s]
                te.wait_ge(sem[name], n)
        if i >= 8:
            te.wait_ge(sem["y%d" % (i - 8)], 1)
        te.matmul_mx(T.ps[:, bank:bank + W], T.kc[:, a:a + W], T.kp[:, a:a + W], T.xqc[:], T.xqp[:],
                     True, True).then_inc(sem["m%d" % i], 1)
        y = T.yb[:, W * s:W * s + W]
        if i % 2 == 0:
            sc.wait_ge(sem["m%d" % i], 1)
            sc.activation(y, T.ps[:, bank:bank + W], ActivationFunctionType.Copy).then_inc(sem["y%d" % i], 1)
        else:
            v.wait_ge(sem["m%d" % i], 1)
            v.tensor_copy(y, T.ps[:, bank:bank + W]).then_inc(sem["y%d" % i], 1)
        q = sc if i >= N - 4 and i % 2 == 0 else g.sync
        q.wait_ge(sem["y%d" % i], 1)
        q.dma_start(T.y[:, W * s:W * s + W], y).then_inc(sem["st"], 16)
    g.sync.wait_ge(sem["st"], 16 * N)
